import numpy as np
import ml_dtypes


def mxq(x, axis, fmt="e4m3"):
    dtype, down = {"e4m3": (ml_dtypes.float8_e4m3fn, 7), "e5m2": (ml_dtypes.float8_e5m2, 14)}[fmt]
    v = np.moveaxis(np.asarray(x, np.float32).astype(ml_dtypes.bfloat16).astype(np.float64), axis, -1)
    blocks = v.reshape(v.shape[:-1] + (-1, 32))
    amax = np.abs(blocks).max(-1, keepdims=True)
    byte = np.maximum(np.where(amax > 0, np.frexp(amax)[1] - 1 + 127, 0) - down, 1)
    scale = np.exp2(byte - 127.0)
    codes = (blocks / scale).astype(np.float32).astype(dtype).astype(np.float64)
    return np.moveaxis((codes * scale).reshape(v.shape), -1, axis)


WIDE = False


def mx_kscale(k):
    if not WIDE:
        return np.ones(k)
    levels = np.array([10, -10, 5, -5, 0])
    if k % 512:
        return np.exp2(np.random.permutation(np.resize(levels, k // 32))).repeat(32)
    a = np.empty((k // 512, 16))
    for p in range(k // 512):
        a[p, :8] = np.random.permutation(np.resize(levels, 8))
        for g in range(8):
            far = levels[np.abs(levels - a[p, g]) >= 10]
            a[p, g + 8] = far[np.random.randint(len(far))]
    return np.exp2(a.ravel()).repeat(32)


def f64(x):
    return np.asarray(x).astype(np.float64)


def striped8(idx):
    return np.asarray(idx).reshape(8, -1, 16).transpose(0, 2, 1).reshape(128, -1).astype(np.uint16)


def unstriped8(offs):
    return offs.reshape(8, 16, -1).transpose(0, 2, 1).reshape(8, -1).astype(np.int64)


def pick8(x, idx, run):
    r = np.arange(len(x))
    return x[r[:, None], idx[r % (8 * run) // run]]


E2M1 = np.array([0.0, 0.5, 1.0, 1.5, 2.0, 3.0, 4.0, 6.0, -0.0, -0.5, -1.0, -1.5, -2.0, -3.0, -4.0, -6.0])


def pack_weight(w, fmt):
    k, n = w.shape
    w = f64(np.asarray(w, np.float32).astype(ml_dtypes.bfloat16)).reshape(k // 32, 32, n)
    amax = np.abs(w).max(1)
    if fmt == "e4m3":
        byte = np.frexp(amax)[1] - 1 + 127 - 7
    else:
        mant, ex = np.frexp(amax / 6.0)
        byte = np.where(mant > 0.5, ex, ex - 1) + 127
    byte = np.clip(np.where(amax > 0, byte, 1), 1, 254)
    scaled = (w * np.exp2(127.0 - byte)[:, None, :]).reshape(k, n).astype(np.float32)
    by_word = np.ascontiguousarray(scaled.reshape(k // 512, 128, 4, n).transpose(0, 1, 3, 2))
    if fmt == "e4m3":
        words = by_word.astype(ml_dtypes.float8_e4m3fn).view(np.uint8)
    else:
        c = by_word.astype(ml_dtypes.float4_e2m1fn).view(np.uint8) & 0xF
        words = (c[..., 0::2] | (c[..., 1::2] << 4)).reshape(k // 512, 128, 2 * n)
    return np.ascontiguousarray(words), np.ascontiguousarray(byte.astype(np.uint8).reshape(k // 512, 16, n))


def unpack_weight(words, scales, fmt):
    g, _, n = scales.shape
    words = np.ascontiguousarray(words).reshape(g, 128, n, -1)
    if fmt == "e4m3":
        vals = words.view(ml_dtypes.float8_e4m3fn).astype(np.float64)
    else:
        nib = np.empty((g, 128, n, 4), np.uint8)
        nib[..., 0::2] = words & 0xF
        nib[..., 1::2] = words >> 4
        vals = E2M1[nib]
    vals = vals * np.repeat(np.exp2(scales.astype(np.float64) - 127.0), 8, axis=1)[..., None]
    return vals.transpose(0, 1, 3, 2).reshape(g * 512, n)


D, V, Q, I = 512, 2048, 128, 512


def setup_inputs():
    n = np.random.standard_normal
    idx = np.stack([np.random.permutation(V)[:I] for _ in range(8)])
    fd = mx_kscale(D)
    vocp = pack_weight(n((D, V)) / fd[:, None], "e2m1")
    return {
        "hid": (n((D, Q)) * 0.7 / np.sqrt(D) * fd[:, None]).astype(np.float32),
        "voc_words": vocp[0],
        "voc_scales": vocp[1],
        "lpo": (np.random.uniform(-8.2, -7.2, (Q, I))).astype(np.float32),
        "adv": (1.0 * n((Q, I))).astype(np.float32),
        "base": (0.3 * n((Q, V))).astype(np.float32),
        "offs": striped8(idx),
    }


def reference(hid, voc_words, voc_scales, lpo, adv, base, offs):
    idx = unstriped8(offs)
    vocu = unpack_weight(voc_words, voc_scales, "e2m1")
    hidq = mxq(f64(hid), 0, "e4m3")
    a = hidq.T @ vocu
    p = np.exp(a)
    z = np.sum(p, axis=1, keepdims=True)
    r = np.exp(pick8(a, idx, 16) - np.log(z) - f64(lpo))
    dz = np.sum(f64(adv) * r * (-1.0), axis=1, keepdims=True) / z
    e1 = f64(adv) * r
    s1 = np.zeros((Q, V))
    s1[np.arange(Q)[:, None], idx[np.arange(Q) % 128 // 16]] = e1
    da = dz * p + s1
    hda = da * 2.0
    he1 = pick8(hda, idx, 16)
    hdz = np.sum(hda * p, axis=1, keepdims=True)
    hr = he1 * f64(adv) + hdz / z * (-1.0) * f64(adv)
    hz = np.sum(hr * r * (-1.0), axis=1, keepdims=True) / z - hdz * np.sum(f64(adv) * r * (-1.0), axis=1, keepdims=True) / np.square(z)
    hp = hda * dz + hz
    e51 = hr * r
    s51 = np.zeros((Q, V))
    s51[np.arange(Q)[:, None], idx[np.arange(Q) % 128 // 16]] = e51
    ha = hp * p + s51
    y = ha + f64(base)
    return y

@@ -1,0 +1,215 @@
+from contextlib import ExitStack
+import math
+
+import concourse.mybir as mybir
+from concourse.masks import make_identity
+
+D, V, Q, I = 512, 2048, 128, 512
+FLOPS = 2 * D * V * Q
+
+F32 = mybir.dt.float32
+BF16 = mybir.dt.bfloat16
+I32 = mybir.dt.int32
+U32 = mybir.dt.uint32
+U16 = mybir.dt.uint16
+U8 = mybir.dt.uint8
+FP8X4 = mybir.dt.float8_e4m3fn_x4
+FP4X4 = mybir.dt.float4_e2m1fn_x4
+ALU = mybir.AluOpType
+ACT = mybir.ActivationFunctionType
+
+P = 128
+BANK = 512
+BANKS = V // BANK
+HALF = V // 2
+TINY = 1e-37
+
+
+def tile_attend_gppolicyratio_heads_kernel(tc, hid, voc_words, voc_scales, lpo, adv, base, offs, out):
+    nc = tc.nc
+    with ExitStack() as ctx:
+        sb = ctx.enter_context(tc.tile_pool(name="sb", bufs=1))
+        ps = ctx.enter_context(tc.psum_pool(name="ps", bufs=1))
+
+        def col(name, width=1):
+            return sb.tile([P, width], F32, name=name)
+
+        def bank_cols(b):
+            return slice(b * BANK, (b + 1) * BANK)
+
+        def half_cols(h):
+            return slice(h * HALF, (h + 1) * HALF)
+
+        v_scales = sb.tile([P, V], U8, name="v_scales", align_bytes=64)
+        nc.gpsimd.memset(v_scales[:].bitcast(I32), 0)
+        listed = sb.tile([P, V], F32, name="listed")
+        nc.vector.memset(listed[:], 0.0)
+
+        hid_raw = sb.tile([P, 4, Q], F32, name="hid_raw")
+        nc.sync.dma_start(out=hid_raw[:], in_=hid.rearrange("(p j) q -> p j q", j=4))
+        for quad in range(4):
+            nc.scalar.dma_start(
+                out=v_scales[32 * quad : 32 * quad + 4, :].bitcast(I32),
+                in_=voc_scales[0, 4 * quad : 4 * quad + 4, :].bitcast(I32),
+            )
+        v_words = []
+        for h in range(2):
+            words = sb.tile([P, 2 * HALF], U8, name="v_words%d" % h, align_bytes=64)
+            nc.sync.dma_start(out=words[:].bitcast(I32), in_=voc_words[0, :, 2 * HALF * h : 2 * HALF * (h + 1)].bitcast(I32))
+            v_words.append(words)
+        offsets = sb.tile([P, I // 16], U16, name="offsets")
+        nc.sync.dma_start(offsets[:], offs)
+
+        minus_half = sb.tile([P, 2], F32, name="minus_half", tag="seed_then_rows")
+        nc.gpsimd.memset(minus_half[:], -0.5)
+        factors = sb.tile([P, 3, 2], F32, name="factors")
+        for row, times in enumerate((1.0, -1.0 / math.sqrt(2.0), 0.75)):
+            nc.gpsimd.tensor_scalar(factors[:, row, :], minus_half[:], times, 0.0, ALU.mult, ALU.add)
+        warm = col("warm")
+        nc.scalar.activation(warm[:], factors[:, 2, 0:1], ACT.Exp)
+        rows_sb = sb.tile([P, 2 * I + V], F32, name="rows_sb", tag="seed_then_rows")
+        lpo_sb = rows_sb[:, 0:I]
+        adv_sb = rows_sb[:, I : 2 * I]
+        nc.sync.dma_start(out=lpo_sb, in_=lpo)
+        nc.sync.dma_start(out=adv_sb, in_=adv)
+        for h in range(2):
+            nc.sync.dma_start(out=rows_sb[:, 2 * I + h * HALF : 2 * I + (h + 1) * HALF], in_=base[:, half_cols(h)])
+        ident = sb.tile([P, P], F32, name="ident")
+        make_identity(nc, ident[:])
+
+        grouped = sb.tile([P, Q, 4], BF16, name="grouped", align_bytes=64)
+        nc.vector.tensor_copy(out=grouped[:], in_=hid_raw[:].rearrange("p j q -> p q j"))
+        h_codes = sb.tile([P, Q], U32, name="h_codes", align_bytes=64)
+        h_scales = sb.tile([P, Q], U8, name="h_scales", align_bytes=64)
+        nc.vector.quantize_mx(out=h_codes[:].bitcast(FP8X4), scales=h_scales[:], in_=grouped[:].rearrange("p q j -> p (q j)"))
+
+        a = sb.tile([P, V], F32, name="a")
+        pieces = [(0, BANK, "rows0"), (BANK, BANK, "rows1"), (2 * BANK, BANK, "rows2"), (3 * BANK, BANK // 2, "rows3"), (3 * BANK + BANK // 2, BANK // 2, "turned3")]
+        piece_max = col("piece_max", len(pieces))
+        for n, (first, width, tag) in enumerate(pieces):
+            acc = ps.tile([P, width], F32, name="acc%d" % n, tag=tag)
+            byte = 2 * (first % HALF)
+            nc.tensor.matmul_mx(
+                out=acc[:],
+                lhsT=h_codes[:].bitcast(FP8X4),
+                lhsT_scale=h_scales[:],
+                rhs=v_words[first // HALF][:, byte : byte + 2 * width].bitcast(FP4X4),
+                rhs_scale=v_scales[:, first : first + width],
+                start=True,
+                stop=True,
+            )
+            nc.vector.tensor_scalar(a[:, first : first + width], acc[:], 1.0, None, ALU.mult, ALU.max, accum_out=piece_max[:, n : n + 1])
+        shift = col("shift", 2)
+        running = col("running", 2)
+        nc.gpsimd.tensor_scalar(shift[:, 0:1], piece_max[:, 0:1], piece_max[:, 1:2], -1.0, ALU.max, ALU.mult)
+        nc.gpsimd.tensor_scalar(running[:, 0:1], piece_max[:, 2:3], -1.0, shift[:, 0:1], ALU.mult, ALU.min)
+        nc.gpsimd.tensor_scalar(running[:, 1:2], piece_max[:, 3:4], -1.0, running[:, 0:1], ALU.mult, ALU.min)
+        nc.gpsimd.tensor_scalar(shift[:, 1:2], piece_max[:, 4:5], -1.0, running[:, 1:2], ALU.mult, ALU.min)
+
+        p = sb.tile([P, V], F32, name="p")
+        z_half = col("z_half", 2)
+        for h in range(2):
+            nc.scalar.activation(p[:, half_cols(h)], a[:, half_cols(h)], ACT.Exp, bias=shift[:, h : h + 1], accum_out=z_half[:, h : h + 1])
+        lift = col("lift", 2)
+        nc.scalar.activation(lift[:], shift[:], ACT.Exp, bias=shift[:, 1:2], scale=-1.0)
+
+        a_i = sb.tile([P, I], F32, name="a_i")
+        nc.vector.tensor_copy(a_i[:], a[:].indirect(offsets[:]))
+        gap = sb.tile([P, I], F32, name="gap")
+        r_raw = sb.tile([P, I], F32, name="r_raw")
+        for h in range(2):
+            part = slice(h * I // 2, (h + 1) * I // 2)
+            nc.vector.tensor_tensor(gap[:, part], a_i[:, part], rows_sb[:, part], ALU.subtract)
+            nc.scalar.activation(r_raw[:, part], gap[:, part], ACT.Exp, bias=shift[:, 1:2])
+        p_i = sb.tile([P, I], F32, name="p_i")
+        nc.scalar.activation(p_i[:], a_i[:], ACT.Exp, bias=shift[:, 1:2])
+
+        z = col("z")
+        z_parts = col("z_parts", 2)
+        nc.vector.scalar_tensor_tensor(z_parts[:], z_half[:], 0.5, lift[:], ALU.mult, ALU.mult, accum_out=z[:])
+        inv_z = col("inv_z")
+        nc.vector.reciprocal(inv_z[:], z[:])
+        e2 = sb.tile([P, I], F32, name="e2")
+        s2 = col("s2")
+        nc.vector.scalar_tensor_tensor(e2[:], r_raw[:], inv_z[:], adv_sb, ALU.mult, ALU.mult, accum_out=s2[:])
+        norms = sb.tile([P, 3, 2], F32, name="norms")
+        nc.vector.scalar_tensor_tensor(norms[:], lift[:].unsqueeze(1).to_broadcast([P, 3, 2]), inv_z[:], factors[:], ALU.mult, ALU.mult)
+
+        scaled = sb.tile([P, 2, 2], F32, name="scaled")
+        nc.scalar.activation(scaled[:], norms[:, 0:2, :], ACT.Copy, scale=s2[:])
+        s2_sq = col("s2_sq")
+        nc.scalar.activation(s2_sq[:], s2[:], ACT.Copy, scale=s2[:], bias=TINY)
+
+        cross = sb.tile([P, I], F32, name="cross")
+        cross_sum = col("cross_sum")
+        nc.vector.scalar_tensor_tensor(cross[:], p_i[:], norms[:, 2, 1:2], e2[:], ALU.mult, ALU.mult, accum_out=cross_sum[:])
+        inv_s2_sq = col("inv_s2_sq")
+        nc.vector.reciprocal(inv_s2_sq[:], s2_sq[:])
+        nc.vector.tensor_copy(listed[:].indirect(offsets[:]), e2[:])
+
+        terms = col("terms", 4)
+        quad_part = sb.tile([P, V], F32, name="quad_part")
+        for h in range(2):
+            nc.scalar.activation(quad_part[:, half_cols(h)], p[:, half_cols(h)], ACT.Square, scale=scaled[:, 1, h : h + 1], accum_out=terms[:, h : h + 1])
+        e1_sq = sb.tile([P, I], F32, name="e1_sq")
+        nc.scalar.activation(e1_sq[:], e2[:], ACT.Square, scale=0.5, accum_out=terms[:, 2:3])
+        nc.scalar.activation(terms[:, 3:4], cross_sum[:], ACT.Copy, scale=s2[:])
+        terms2 = col("terms2", 4)
+        w2 = col("w2")
+        nc.scalar.activation(terms2[:], terms[:], ACT.Copy, scale=2.0, accum_out=w2[:])
+        lin_scale = col("lin_scale", 2)
+        nc.scalar.activation(lin_scale[:], norms[:, 0, :], ACT.Copy, scale=w2[:])
+        inv_s2 = col("inv_s2")
+        nc.scalar.activation(inv_s2[:], inv_s2_sq[:], ACT.Copy, scale=s2[:])
+        sq_parts = col("sq_parts", 2)
+        sq_sum = col("sq_sum")
+        nc.scalar.activation(sq_parts[:], terms[:, 0:2], ACT.Copy, scale=inv_s2[:], accum_out=sq_sum[:])
+        neg_half_c = col("neg_half_c")
+        nc.scalar.activation(neg_half_c[:], cross_sum[:], ACT.Identity, scale=2.0 / 3.0, bias=sq_sum[:])
+        offset_i = sb.tile([P, I], F32, name="offset_i")
+        nc.scalar.activation(offset_i[:], e2[:], ACT.Identity, scale=-0.5, bias=neg_half_c[:])
+
+        hda = sb.tile([P, V], F32, name="hda")
+        for h in range(2):
+            nc.vector.scalar_tensor_tensor(hda[:, half_cols(h)], p[:, half_cols(h)], scaled[:, 0, h : h + 1], listed[:, half_cols(h)], ALU.mult, ALU.add)
+        looked = sb.tile([P, I], F32, name="looked")
+        nc.vector.tensor_tensor(looked[:], hda[:].indirect(offsets[:]), offset_i[:], ALU.add)
+        nc.vector.tensor_tensor(listed[:].indirect(offsets[:]), looked[:], e2[:], ALU.mult)
+
+        turned = [ps.tile([P, BANK], F32, name="turned%d" % b, tag="turned%d" % b) for b in range(BANKS)]
+
+        def add_turned(b, source, first, start, stop):
+            for j in range(4):
+                nc.tensor.matmul(
+                    turned[b][:, j * P : (j + 1) * P],
+                    source[:, first + j * P : first + (j + 1) * P],
+                    ident[:],
+                    start=(start and j == 0),
+                    stop=(stop and j == 3),
+                    is_transpose=True,
+                )
+
+        for b in range(BANKS):
+            add_turned(b, rows_sb, 2 * I + b * BANK, True, False)
+        for b in range(BANKS):
+            add_turned(b, quad_part, b * BANK, False, False)
+        lin_part = sb.tile([P, V], F32, name="lin_part")
+        dense = []
+        for b in range(BANKS):
+            nc.scalar.activation(lin_part[:, bank_cols(b)], p[:, bank_cols(b)], ACT.Copy, scale=lin_scale[:, b // 2 : b // 2 + 1])
+            add_turned(b, lin_part, b * BANK, False, True)
+        for b in range(BANKS):
+            turned_sb = sb.tile([P, BANK], F32, name="turned_sb%d" % b)
+            nc.scalar.copy(turned_sb[:], turned[b][:])
+            rows = ps.tile([P, BANK], F32, name="dense%d" % b, tag="rows%d" % b)
+            for j in range(4):
+                nc.tensor.transpose(rows[:, j * P : (j + 1) * P], turned_sb[:, j * P : (j + 1) * P], ident[:])
+            dense.append(rows)
+
+        for n in range(2 * BANKS):
+            width = BANK // 2
+            cols = slice(n * width, (n + 1) * width)
+            result = sb.tile([P, width], F32, name="result%d" % n)
+            nc.vector.tensor_tensor(result[:], dense[n // 2][:, (n % 2) * width : (n % 2 + 1) * width], listed[:, cols], ALU.add)
+            queue = nc.sync if n % 2 == 0 else nc.scalar
+            queue.dma_start(out=out[:, cols], in_=result[:])

@@ -23,6 +23,7 @@ BANK = 512
 BANKS = V // BANK
 HALF = V // 2
 TINY = 1e-37
+STORE_WIDTHS = (256, 256, 512, 512, 256, 256)
 
 
 def tile_attend_gppolicyratio_heads_kernel(tc, hid, voc_words, voc_scales, lpo, adv, base, offs, out):
@@ -42,39 +43,40 @@ def tile_attend_gppolicyratio_heads_kernel(tc, hid, voc_words, voc_scales, lpo, 
 
         v_scales = sb.tile([P, V], U8, name="v_scales", align_bytes=64)
         nc.gpsimd.memset(v_scales[:].bitcast(I32), 0)
+        minus_half = sb.tile([P, BANKS], F32, name="minus_half", tag="seed_then_words", align_bytes=64)
+        nc.gpsimd.memset(minus_half[:], -0.5)
+        factors = sb.tile([P, 2, BANKS], F32, name="factors")
+        nc.gpsimd.tensor_scalar(factors[:, 0, :], minus_half[:], 1.0, 0.0, ALU.mult, ALU.add)
+        seed = sb.tile([P, BANKS], F32, name="seed", tag="seed_then_rows")
+        nc.gpsimd.memset(seed[:], 0.5)
+        nc.gpsimd.tensor_scalar(factors[:, 1, :], seed[:], 1.0 / math.sqrt(2.0), 0.0, ALU.mult, ALU.add)
         listed = sb.tile([P, V], F32, name="listed")
         nc.vector.memset(listed[:], 0.0)
 
         hid_raw = sb.tile([P, 4, Q], F32, name="hid_raw")
         nc.sync.dma_start(out=hid_raw[:], in_=hid.rearrange("(p j) q -> p j q", j=4))
-        for quad in range(4):
-            nc.scalar.dma_start(
-                out=v_scales[32 * quad : 32 * quad + 4, :].bitcast(I32),
-                in_=voc_scales[0, 4 * quad : 4 * quad + 4, :].bitcast(I32),
-            )
-        v_words = []
-        for h in range(2):
-            words = sb.tile([P, 2 * HALF], U8, name="v_words%d" % h, align_bytes=64)
-            nc.sync.dma_start(out=words[:].bitcast(I32), in_=voc_words[0, :, 2 * HALF * h : 2 * HALF * (h + 1)].bitcast(I32))
-            v_words.append(words)
         offsets = sb.tile([P, I // 16], U16, name="offsets")
         nc.sync.dma_start(offsets[:], offs)
-
-        minus_half = sb.tile([P, 2], F32, name="minus_half", tag="seed_then_rows")
-        nc.gpsimd.memset(minus_half[:], -0.5)
-        factors = sb.tile([P, 3, 2], F32, name="factors")
-        for row, times in enumerate((1.0, -1.0 / math.sqrt(2.0), 0.75)):
-            nc.gpsimd.tensor_scalar(factors[:, row, :], minus_half[:], times, 0.0, ALU.mult, ALU.add)
-        warm = col("warm")
-        nc.scalar.activation(warm[:], factors[:, 2, 0:1], ACT.Exp)
+        for row in range(4):
+            nc.sync.dma_start(
+                out=v_scales[row:P:32, :].bitcast(I32),
+                in_=voc_scales[0, row:16:4, :].bitcast(I32),
+            )
+        v_words = sb.tile([P, 2 * V], U8, name="v_words", tag="seed_then_words", align_bytes=64)
+        for h in range(2):
+            nc.sync.dma_start(out=v_words[:, V * h : V * (h + 1)].bitcast(I32), in_=voc_words[0, :, V * h : V * (h + 1)].bitcast(I32))
         rows_sb = sb.tile([P, 2 * I + V], F32, name="rows_sb", tag="seed_then_rows")
-        lpo_sb = rows_sb[:, 0:I]
         adv_sb = rows_sb[:, I : 2 * I]
-        nc.sync.dma_start(out=lpo_sb, in_=lpo)
+        nc.sync.dma_start(out=rows_sb[:, 0:I], in_=lpo)
         nc.sync.dma_start(out=adv_sb, in_=adv)
         for h in range(2):
             nc.sync.dma_start(out=rows_sb[:, 2 * I + h * HALF : 2 * I + (h + 1) * HALF], in_=base[:, half_cols(h)])
+
+        warm = col("warm")
+        nc.scalar.activation(warm[:], factors[:, 0, 0:1], ACT.Exp)
         ident = sb.tile([P, P], F32, name="ident")
+        minus_one = col("minus_one")
+        nc.gpsimd.memset(minus_one[:], -1.0)
         make_identity(nc, ident[:])
 
         grouped = sb.tile([P, Q, 4], BF16, name="grouped", align_bytes=64)
@@ -84,94 +86,104 @@ def tile_attend_gppolicyratio_heads_kernel(tc, hid, voc_words, voc_scales, lpo, 
         nc.vector.quantize_mx(out=h_codes[:].bitcast(FP8X4), scales=h_scales[:], in_=grouped[:].rearrange("p q j -> p (q j)"))
 
         a = sb.tile([P, V], F32, name="a")
-        pieces = [(0, BANK, "rows0"), (BANK, BANK, "rows1"), (2 * BANK, BANK, "rows2"), (3 * BANK, BANK // 2, "rows3"), (3 * BANK + BANK // 2, BANK // 2, "turned3")]
+        pieces = [(0, BANK // 2, "rows0"), (BANK // 2, BANK // 2, "turned3"), (BANK, BANK, "rows1"), (2 * BANK, BANK, "rows2"), (3 * BANK, BANK, "rows3")]
         piece_max = col("piece_max", len(pieces))
         for n, (first, width, tag) in enumerate(pieces):
             acc = ps.tile([P, width], F32, name="acc%d" % n, tag=tag)
-            byte = 2 * (first % HALF)
             nc.tensor.matmul_mx(
                 out=acc[:],
                 lhsT=h_codes[:].bitcast(FP8X4),
                 lhsT_scale=h_scales[:],
-                rhs=v_words[first // HALF][:, byte : byte + 2 * width].bitcast(FP4X4),
+                rhs=v_words[:, 2 * first : 2 * (first + width)].bitcast(FP4X4),
                 rhs_scale=v_scales[:, first : first + width],
                 start=True,
                 stop=True,
             )
             nc.vector.tensor_scalar(a[:, first : first + width], acc[:], 1.0, None, ALU.mult, ALU.max, accum_out=piece_max[:, n : n + 1])
-        shift = col("shift", 2)
-        running = col("running", 2)
+        shift = col("shift", BANKS)
         nc.gpsimd.tensor_scalar(shift[:, 0:1], piece_max[:, 0:1], piece_max[:, 1:2], -1.0, ALU.max, ALU.mult)
-        nc.gpsimd.tensor_scalar(running[:, 0:1], piece_max[:, 2:3], -1.0, shift[:, 0:1], ALU.mult, ALU.min)
-        nc.gpsimd.tensor_scalar(running[:, 1:2], piece_max[:, 3:4], -1.0, running[:, 0:1], ALU.mult, ALU.min)
-        nc.gpsimd.tensor_scalar(shift[:, 1:2], piece_max[:, 4:5], -1.0, running[:, 1:2], ALU.mult, ALU.min)
+        for b in range(1, BANKS):
+            nc.gpsimd.tensor_scalar(shift[:, b : b + 1], piece_max[:, b + 1 : b + 2], -1.0, shift[:, b - 1 : b], ALU.mult, ALU.min)
+        row_shift = shift[:, BANKS - 1 : BANKS]
 
         p = sb.tile([P, V], F32, name="p")
-        z_half = col("z_half", 2)
-        for h in range(2):
-            nc.scalar.activation(p[:, half_cols(h)], a[:, half_cols(h)], ACT.Exp, bias=shift[:, h : h + 1], accum_out=z_half[:, h : h + 1])
-        lift = col("lift", 2)
-        nc.scalar.activation(lift[:], shift[:], ACT.Exp, bias=shift[:, 1:2], scale=-1.0)
+        z_bank = col("z_bank", BANKS)
+        for b in range(BANKS):
+            nc.scalar.activation(p[:, bank_cols(b)], a[:, bank_cols(b)], ACT.Exp, bias=shift[:, b : b + 1], accum_out=z_bank[:, b : b + 1])
+        lift = col("lift", BANKS)
+        nc.scalar.activation(lift[:], shift[:], ACT.Exp, bias=row_shift, scale=-1.0)
 
         a_i = sb.tile([P, I], F32, name="a_i")
         nc.vector.tensor_copy(a_i[:], a[:].indirect(offsets[:]))
-        gap = sb.tile([P, I], F32, name="gap")
+        gap = sb.tile([P, I], F32, name="gap", tag="gap_then_p_i")
         r_raw = sb.tile([P, I], F32, name="r_raw")
-        for h in range(2):
-            part = slice(h * I // 2, (h + 1) * I // 2)
+        parts = [slice(h * I // 2, (h + 1) * I // 2) for h in range(2)]
+
+        def ratio(part):
             nc.vector.tensor_tensor(gap[:, part], a_i[:, part], rows_sb[:, part], ALU.subtract)
-            nc.scalar.activation(r_raw[:, part], gap[:, part], ACT.Exp, bias=shift[:, 1:2])
-        p_i = sb.tile([P, I], F32, name="p_i")
-        nc.scalar.activation(p_i[:], a_i[:], ACT.Exp, bias=shift[:, 1:2])
+            nc.scalar.activation(r_raw[:, part], gap[:, part], ACT.Exp, bias=row_shift)
 
-        z = col("z")
-        z_parts = col("z_parts", 2)
-        nc.vector.scalar_tensor_tensor(z_parts[:], z_half[:], 0.5, lift[:], ALU.mult, ALU.mult, accum_out=z[:])
-        inv_z = col("inv_z")
-        nc.vector.reciprocal(inv_z[:], z[:])
+        ratio(parts[0])
+        half_z = col("half_z")
+        z_parts = col("z_parts", BANKS)
+        nc.vector.scalar_tensor_tensor(z_parts[:], z_bank[:], 0.5, lift[:], ALU.mult, ALU.mult, accum_out=half_z[:])
+        ratio(parts[1])
+        two_by_z = col("two_by_z")
+        nc.vector.reciprocal(two_by_z[:], half_z[:])
         e2 = sb.tile([P, I], F32, name="e2")
+        s2_parts = col("s2_parts", 2)
+        for h, part in enumerate(parts):
+            nc.vector.scalar_tensor_tensor(e2[:, part], r_raw[:, part], two_by_z[:], rows_sb[:, I + part.start : I + part.stop], ALU.mult, ALU.mult, accum_out=s2_parts[:, h : h + 1])
+        p_i = sb.tile([P, I], F32, name="p_i", tag="gap_then_p_i")
+        nc.scalar.activation(p_i[:], a_i[:], ACT.Exp, bias=row_shift)
         s2 = col("s2")
-        nc.vector.scalar_tensor_tensor(e2[:], r_raw[:], inv_z[:], adv_sb, ALU.mult, ALU.mult, accum_out=s2[:])
-        norms = sb.tile([P, 3, 2], F32, name="norms")
-        nc.vector.scalar_tensor_tensor(norms[:], lift[:].unsqueeze(1).to_broadcast([P, 3, 2]), inv_z[:], factors[:], ALU.mult, ALU.mult)
-
-        scaled = sb.tile([P, 2, 2], F32, name="scaled")
-        nc.scalar.activation(scaled[:], norms[:, 0:2, :], ACT.Copy, scale=s2[:])
-        s2_sq = col("s2_sq")
-        nc.scalar.activation(s2_sq[:], s2[:], ACT.Copy, scale=s2[:], bias=TINY)
-
-        cross = sb.tile([P, I], F32, name="cross")
-        cross_sum = col("cross_sum")
-        nc.vector.scalar_tensor_tensor(cross[:], p_i[:], norms[:, 2, 1:2], e2[:], ALU.mult, ALU.mult, accum_out=cross_sum[:])
-        inv_s2_sq = col("inv_s2_sq")
-        nc.vector.reciprocal(inv_s2_sq[:], s2_sq[:])
+        nc.scalar.activation(s2[:], s2_parts[:, 0:1], ACT.Identity, bias=s2_parts[:, 1:2])
+        lifted = sb.tile([P, 2, BANKS], F32, name="lifted")
+        nc.gpsimd.tensor_tensor(lifted[:], lift[:].unsqueeze(1).to_broadcast([P, 2, BANKS]), factors[:], ALU.mult)
+        norms = sb.tile([P, 2, BANKS], F32, name="norms")
+        nc.scalar.activation(norms[:], lifted[:], ACT.Copy, scale=two_by_z[:])
         nc.vector.tensor_copy(listed[:].indirect(offsets[:]), e2[:])
 
-        terms = col("terms", 4)
-        quad_part = sb.tile([P, V], F32, name="quad_part")
-        for h in range(2):
-            nc.scalar.activation(quad_part[:, half_cols(h)], p[:, half_cols(h)], ACT.Square, scale=scaled[:, 1, h : h + 1], accum_out=terms[:, h : h + 1])
-        e1_sq = sb.tile([P, I], F32, name="e1_sq")
-        nc.scalar.activation(e1_sq[:], e2[:], ACT.Square, scale=0.5, accum_out=terms[:, 2:3])
-        nc.scalar.activation(terms[:, 3:4], cross_sum[:], ACT.Copy, scale=s2[:])
-        terms2 = col("terms2", 4)
-        w2 = col("w2")
-        nc.scalar.activation(terms2[:], terms[:], ACT.Copy, scale=2.0, accum_out=w2[:])
-        lin_scale = col("lin_scale", 2)
-        nc.scalar.activation(lin_scale[:], norms[:, 0, :], ACT.Copy, scale=w2[:])
+        s2_sq = col("s2_sq")
+        nc.gpsimd.tensor_scalar(s2_sq[:], s2[:], s2[:], TINY, ALU.mult, ALU.add)
+        inv_s2_sq = col("inv_s2_sq")
+        nc.gpsimd.tensor_tensor(inv_s2_sq[:], s2_sq[:], minus_one[:], ALU.pow)
         inv_s2 = col("inv_s2")
-        nc.scalar.activation(inv_s2[:], inv_s2_sq[:], ACT.Copy, scale=s2[:])
-        sq_parts = col("sq_parts", 2)
+        nc.gpsimd.tensor_scalar(inv_s2[:], inv_s2_sq[:], s2[:], 0.0, ALU.mult, ALU.add)
+        s2_34 = col("s2_34")
+        nc.gpsimd.tensor_scalar(s2_34[:], s2[:], 0.75, 0.0, ALU.mult, ALU.add)
+        cross = sb.tile([P, I], F32, name="cross")
+        nc.gpsimd.tensor_tensor(cross[:], p_i[:], e2[:], ALU.mult)
+
+        scaled = sb.tile([P, 2, BANKS], F32, name="scaled")
+        nc.scalar.activation(scaled[:], norms[:], ACT.Copy, scale=s2[:])
+
+        terms = col("terms", BANKS + 2)
+        quad_part = sb.tile([P, V], F32, name="quad_part")
+        for b in range(BANKS):
+            nc.scalar.activation(quad_part[:, bank_cols(b)], p[:, bank_cols(b)], ACT.Square, scale=scaled[:, 1, b : b + 1], accum_out=terms[:, b : b + 1])
+        cross_n = sb.tile([P, I], F32, name="cross_n")
+        neg_p2 = col("neg_p2")
+        nc.scalar.activation(cross_n[:], cross[:], ACT.Copy, scale=norms[:, 0, BANKS - 1 : BANKS], accum_out=neg_p2[:])
+        sq_parts = col("sq_parts", BANKS)
         sq_sum = col("sq_sum")
-        nc.scalar.activation(sq_parts[:], terms[:, 0:2], ACT.Copy, scale=inv_s2[:], accum_out=sq_sum[:])
-        neg_half_c = col("neg_half_c")
-        nc.scalar.activation(neg_half_c[:], cross_sum[:], ACT.Identity, scale=2.0 / 3.0, bias=sq_sum[:])
+        nc.scalar.activation(sq_parts[:], terms[:, 0:BANKS], ACT.Copy, scale=inv_s2[:], accum_out=sq_sum[:])
+        neg_half_c = sb.tile([P, 1], F32, name="neg_half_c", tag="c_then_squares")
+        nc.scalar.activation(neg_half_c[:], neg_p2[:], ACT.Identity, scale=0.5, bias=sq_sum[:])
         offset_i = sb.tile([P, I], F32, name="offset_i")
         nc.scalar.activation(offset_i[:], e2[:], ACT.Identity, scale=-0.5, bias=neg_half_c[:])
+        e1_sq = sb.tile([P, I], F32, name="e1_sq", tag="c_then_squares")
+        nc.scalar.activation(e1_sq[:], e2[:], ACT.Square, scale=0.5, accum_out=terms[:, BANKS : BANKS + 1])
+        nc.scalar.activation(terms[:, BANKS + 1 : BANKS + 2], neg_p2[:], ACT.Copy, scale=s2_34[:])
+        terms2 = col("terms2", BANKS + 2)
+        w2 = col("w2")
+        nc.scalar.activation(terms2[:], terms[:], ACT.Copy, scale=2.0, accum_out=w2[:])
+        lin_scale = col("lin_scale", BANKS)
+        nc.scalar.activation(lin_scale[:], norms[:, 0, :], ACT.Copy, scale=w2[:])
 
         hda = sb.tile([P, V], F32, name="hda")
-        for h in range(2):
-            nc.vector.scalar_tensor_tensor(hda[:, half_cols(h)], p[:, half_cols(h)], scaled[:, 0, h : h + 1], listed[:, half_cols(h)], ALU.mult, ALU.add)
+        for b in range(BANKS):
+            nc.vector.scalar_tensor_tensor(hda[:, bank_cols(b)], p[:, bank_cols(b)], scaled[:, 0, b : b + 1], listed[:, bank_cols(b)], ALU.mult, ALU.add)
         looked = sb.tile([P, I], F32, name="looked")
         nc.vector.tensor_tensor(looked[:], hda[:].indirect(offsets[:]), offset_i[:], ALU.add)
         nc.vector.tensor_tensor(listed[:].indirect(offsets[:]), looked[:], e2[:], ALU.mult)
@@ -196,7 +208,7 @@ def tile_attend_gppolicyratio_heads_kernel(tc, hid, voc_words, voc_scales, lpo, 
         lin_part = sb.tile([P, V], F32, name="lin_part")
         dense = []
         for b in range(BANKS):
-            nc.scalar.activation(lin_part[:, bank_cols(b)], p[:, bank_cols(b)], ACT.Copy, scale=lin_scale[:, b // 2 : b // 2 + 1])
+            nc.scalar.activation(lin_part[:, bank_cols(b)], p[:, bank_cols(b)], ACT.Copy, scale=lin_scale[:, b : b + 1])
             add_turned(b, lin_part, b * BANK, False, True)
         for b in range(BANKS):
             turned_sb = sb.tile([P, BANK], F32, name="turned_sb%d" % b)
@@ -206,10 +218,11 @@ def tile_attend_gppolicyratio_heads_kernel(tc, hid, voc_words, voc_scales, lpo, 
                 nc.tensor.transpose(rows[:, j * P : (j + 1) * P], turned_sb[:, j * P : (j + 1) * P], ident[:])
             dense.append(rows)
 
-        for n in range(2 * BANKS):
-            width = BANK // 2
-            cols = slice(n * width, (n + 1) * width)
+        first = 0
+        for n, width in enumerate(STORE_WIDTHS):
+            cols = slice(first, first + width)
             result = sb.tile([P, width], F32, name="result%d" % n)
-            nc.vector.tensor_tensor(result[:], dense[n // 2][:, (n % 2) * width : (n % 2 + 1) * width], listed[:, cols], ALU.add)
+            nc.vector.tensor_tensor(result[:], dense[first // BANK][:, first % BANK : first % BANK + width], listed[:, cols], ALU.add)
             queue = nc.sync if n % 2 == 0 else nc.scalar
             queue.dma_start(out=out[:, cols], in_=result[:])
+            first = first + width

@@ -42,15 +42,16 @@ def tile_attend_gppolicyratio_heads_kernel(tc, hid, voc_words, voc_scales, lpo, 
             return slice(h * HALF, (h + 1) * HALF)
 
         v_scales = sb.tile([P, V], U8, name="v_scales", align_bytes=64)
-        nc.gpsimd.memset(v_scales[:].bitcast(I32), 0)
-        minus_half = sb.tile([P, BANKS], F32, name="minus_half", tag="seed_then_words", align_bytes=64)
-        nc.gpsimd.memset(minus_half[:], -0.5)
-        factors = sb.tile([P, 2, BANKS], F32, name="factors")
-        nc.gpsimd.tensor_scalar(factors[:, 0, :], minus_half[:], 1.0, 0.0, ALU.mult, ALU.add)
-        seed = sb.tile([P, BANKS], F32, name="seed", tag="seed_then_rows")
-        nc.gpsimd.memset(seed[:], 0.5)
-        nc.gpsimd.tensor_scalar(factors[:, 1, :], seed[:], 1.0 / math.sqrt(2.0), 0.0, ALU.mult, ALU.add)
-        listed = sb.tile([P, V], F32, name="listed")
+        nc.vector.memset(v_scales[:].bitcast(I32), 0)
+        plus = sb.tile([P, 1], F32, name="plus", tag="seed_then_words", align_bytes=64)
+        nc.vector.memset(plus[:], 1.0)
+        minus = sb.tile([P, 1], F32, name="minus", tag="seed_then_listed")
+        nc.vector.memset(minus[:], -1.0)
+        minus_one = col("minus_one")
+        nc.vector.tensor_tensor(minus_one[:], plus[:], minus[:], ALU.mult)
+        warm = sb.tile([P, 1], F32, name="warm", tag="warm_then_rows")
+        nc.scalar.activation(warm[:], minus_one[:], ACT.Exp)
+        listed = sb.tile([P, V], F32, name="listed", tag="seed_then_listed")
         nc.vector.memset(listed[:], 0.0)
 
         hid_raw = sb.tile([P, 4, Q], F32, name="hid_raw")
@@ -65,25 +66,24 @@ def tile_attend_gppolicyratio_heads_kernel(tc, hid, voc_words, voc_scales, lpo, 
         v_words = sb.tile([P, 2 * V], U8, name="v_words", tag="seed_then_words", align_bytes=64)
         for h in range(2):
             nc.sync.dma_start(out=v_words[:, V * h : V * (h + 1)].bitcast(I32), in_=voc_words[0, :, V * h : V * (h + 1)].bitcast(I32))
-        rows_sb = sb.tile([P, 2 * I + V], F32, name="rows_sb", tag="seed_then_rows")
+        rows_sb = sb.tile([P, 2 * I + V], F32, name="rows_sb", tag="warm_then_rows")
         adv_sb = rows_sb[:, I : 2 * I]
         nc.sync.dma_start(out=rows_sb[:, 0:I], in_=lpo)
         nc.sync.dma_start(out=adv_sb, in_=adv)
         for h in range(2):
             nc.sync.dma_start(out=rows_sb[:, 2 * I + h * HALF : 2 * I + (h + 1) * HALF], in_=base[:, half_cols(h)])
 
-        warm = col("warm")
-        nc.scalar.activation(warm[:], factors[:, 0, 0:1], ACT.Exp)
-        ident = sb.tile([P, P], F32, name="ident")
-        minus_one = col("minus_one")
-        nc.gpsimd.memset(minus_one[:], -1.0)
-        make_identity(nc, ident[:])
 
-        grouped = sb.tile([P, Q, 4], BF16, name="grouped", align_bytes=64)
-        nc.vector.tensor_copy(out=grouped[:], in_=hid_raw[:].rearrange("p j q -> p q j"))
+        grouped = sb.tile([P, Q, 4], BF16, name="grouped", tag="grouped_then_ident", align_bytes=64)
         h_codes = sb.tile([P, Q], U32, name="h_codes", align_bytes=64)
         h_scales = sb.tile([P, Q], U8, name="h_scales", align_bytes=64)
-        nc.vector.quantize_mx(out=h_codes[:].bitcast(FP8X4), scales=h_scales[:], in_=grouped[:].rearrange("p q j -> p (q j)"))
+        row_halves = [slice(h * Q // 2, (h + 1) * Q // 2) for h in range(2)]
+        for rows in row_halves:
+            nc.vector.tensor_copy(out=grouped[:, rows, :], in_=hid_raw[:, :, rows].rearrange("p j q -> p q j"))
+        for rows in row_halves:
+            nc.vector.quantize_mx(out=h_codes[:, rows].bitcast(FP8X4), scales=h_scales[:, rows], in_=grouped[:, rows, :].rearrange("p q j -> p (q j)"))
+        ident = sb.tile([P, P], F32, name="ident", tag="grouped_then_ident", align_bytes=64)
+        make_identity(nc, ident[:])
 
         a = sb.tile([P, V], F32, name="a")
         pieces = [(0, BANK // 2, "rows0"), (BANK // 2, BANK // 2, "turned3"), (BANK, BANK, "rows1"), (2 * BANK, BANK, "rows2"), (3 * BANK, BANK, "rows3")]
@@ -139,7 +139,8 @@ def tile_attend_gppolicyratio_heads_kernel(tc, hid, voc_words, voc_scales, lpo, 
         s2 = col("s2")
         nc.scalar.activation(s2[:], s2_parts[:, 0:1], ACT.Identity, bias=s2_parts[:, 1:2])
         lifted = sb.tile([P, 2, BANKS], F32, name="lifted")
-        nc.gpsimd.tensor_tensor(lifted[:], lift[:].unsqueeze(1).to_broadcast([P, 2, BANKS]), factors[:], ALU.mult)
+        nc.gpsimd.tensor_scalar(lifted[:, 0, :], lift[:], -0.5, 0.0, ALU.mult, ALU.add)
+        nc.gpsimd.tensor_scalar(lifted[:, 1, :], lift[:], 0.5 / math.sqrt(2.0), 0.0, ALU.mult, ALU.add)
         norms = sb.tile([P, 2, BANKS], F32, name="norms")
         nc.scalar.activation(norms[:], lifted[:], ACT.Copy, scale=two_by_z[:])
         nc.vector.tensor_copy(listed[:].indirect(offsets[:]), e2[:])

from contextlib import ExitStack
import math

import concourse.mybir as mybir
from concourse.masks import make_identity

D, V, Q, I = 512, 2048, 128, 512
FLOPS = 2 * D * V * Q

F32 = mybir.dt.float32
BF16 = mybir.dt.bfloat16
I32 = mybir.dt.int32
U32 = mybir.dt.uint32
U16 = mybir.dt.uint16
U8 = mybir.dt.uint8
FP8X4 = mybir.dt.float8_e4m3fn_x4
FP4X4 = mybir.dt.float4_e2m1fn_x4
ALU = mybir.AluOpType
ACT = mybir.ActivationFunctionType

P = 128
BANK = 512
BANKS = V // BANK
HALF = V // 2
TINY = 1e-37
STORE_WIDTHS = (256, 256, 512, 512, 256, 256)


def tile_attend_gppolicyratio_heads_kernel(tc, hid, voc_words, voc_scales, lpo, adv, base, offs, out):
    nc = tc.nc
    with ExitStack() as ctx:
        sb = ctx.enter_context(tc.tile_pool(name="sb", bufs=1))
        ps = ctx.enter_context(tc.psum_pool(name="ps", bufs=1))

        def col(name, width=1):
            return sb.tile([P, width], F32, name=name)

        def bank_cols(b):
            return slice(b * BANK, (b + 1) * BANK)

        def half_cols(h):
            return slice(h * HALF, (h + 1) * HALF)

        v_scales = sb.tile([P, V], U8, name="v_scales", align_bytes=64)
        nc.vector.memset(v_scales[:].bitcast(I32), 0)
        plus = sb.tile([P, 1], F32, name="plus", tag="seed_then_words", align_bytes=64)
        nc.vector.memset(plus[:], 1.0)
        minus = sb.tile([P, 1], F32, name="minus", tag="seed_then_listed")
        nc.vector.memset(minus[:], -1.0)
        minus_one = col("minus_one")
        nc.vector.tensor_tensor(minus_one[:], plus[:], minus[:], ALU.mult)
        warm = sb.tile([P, 1], F32, name="warm", tag="warm_then_rows")
        nc.scalar.activation(warm[:], minus_one[:], ACT.Exp)
        listed = sb.tile([P, V], F32, name="listed", tag="seed_then_listed")
        nc.vector.memset(listed[:], 0.0)

        hid_raw = sb.tile([P, 4, Q], F32, name="hid_raw")
        nc.sync.dma_start(out=hid_raw[:], in_=hid.rearrange("(p j) q -> p j q", j=4))
        offsets = sb.tile([P, I // 16], U16, name="offsets")
        nc.sync.dma_start(offsets[:], offs)
        for row in range(4):
            nc.sync.dma_start(
                out=v_scales[row:P:32, :].bitcast(I32),
                in_=voc_scales[0, row:16:4, :].bitcast(I32),
            )
        v_words = sb.tile([P, 2 * V], U8, name="v_words", tag="seed_then_words", align_bytes=64)
        for h in range(2):
            nc.sync.dma_start(out=v_words[:, V * h : V * (h + 1)].bitcast(I32), in_=voc_words[0, :, V * h : V * (h + 1)].bitcast(I32))
        rows_sb = sb.tile([P, 2 * I + V], F32, name="rows_sb", tag="warm_then_rows")
        adv_sb = rows_sb[:, I : 2 * I]
        nc.sync.dma_start(out=rows_sb[:, 0:I], in_=lpo)
        nc.sync.dma_start(out=adv_sb, in_=adv)
        for h in range(2):
            nc.sync.dma_start(out=rows_sb[:, 2 * I + h * HALF : 2 * I + (h + 1) * HALF], in_=base[:, half_cols(h)])


        grouped = sb.tile([P, Q, 4], BF16, name="grouped", tag="grouped_then_ident", align_bytes=64)
        h_codes = sb.tile([P, Q], U32, name="h_codes", align_bytes=64)
        h_scales = sb.tile([P, Q], U8, name="h_scales", align_bytes=64)
        row_halves = [slice(h * Q // 2, (h + 1) * Q // 2) for h in range(2)]
        for rows in row_halves:
            nc.vector.tensor_copy(out=grouped[:, rows, :], in_=hid_raw[:, :, rows].rearrange("p j q -> p q j"))
        for rows in row_halves:
            nc.vector.quantize_mx(out=h_codes[:, rows].bitcast(FP8X4), scales=h_scales[:, rows], in_=grouped[:, rows, :].rearrange("p q j -> p (q j)"))
        ident = sb.tile([P, P], F32, name="ident", tag="grouped_then_ident", align_bytes=64)
        make_identity(nc, ident[:])

        a = sb.tile([P, V], F32, name="a")
        pieces = [(0, BANK // 2, "rows0"), (BANK // 2, BANK // 2, "turned3"), (BANK, BANK, "rows1"), (2 * BANK, BANK, "rows2"), (3 * BANK, BANK, "rows3")]
        piece_max = col("piece_max", len(pieces))
        for n, (first, width, tag) in enumerate(pieces):
            acc = ps.tile([P, width], F32, name="acc%d" % n, tag=tag)
            nc.tensor.matmul_mx(
                out=acc[:],
                lhsT=h_codes[:].bitcast(FP8X4),
                lhsT_scale=h_scales[:],
                rhs=v_words[:, 2 * first : 2 * (first + width)].bitcast(FP4X4),
                rhs_scale=v_scales[:, first : first + width],
                start=True,
                stop=True,
            )
            nc.vector.tensor_scalar(a[:, first : first + width], acc[:], 1.0, None, ALU.mult, ALU.max, accum_out=piece_max[:, n : n + 1])
        shift = col("shift", BANKS)
        nc.gpsimd.tensor_scalar(shift[:, 0:1], piece_max[:, 0:1], piece_max[:, 1:2], -1.0, ALU.max, ALU.mult)
        for b in range(1, BANKS):
            nc.gpsimd.tensor_scalar(shift[:, b : b + 1], piece_max[:, b + 1 : b + 2], -1.0, shift[:, b - 1 : b], ALU.mult, ALU.min)
        row_shift = shift[:, BANKS - 1 : BANKS]

        p = sb.tile([P, V], F32, name="p")
        z_bank = col("z_bank", BANKS)
        for b in range(BANKS):
            nc.scalar.activation(p[:, bank_cols(b)], a[:, bank_cols(b)], ACT.Exp, bias=shift[:, b : b + 1], accum_out=z_bank[:, b : b + 1])
        lift = col("lift", BANKS)
        nc.scalar.activation(lift[:], shift[:], ACT.Exp, bias=row_shift, scale=-1.0)

        a_i = sb.tile([P, I], F32, name="a_i")
        nc.vector.tensor_copy(a_i[:], a[:].indirect(offsets[:]))
        gap = sb.tile([P, I], F32, name="gap", tag="gap_then_p_i")
        r_raw = sb.tile([P, I], F32, name="r_raw")
        parts = [slice(h * I // 2, (h + 1) * I // 2) for h in range(2)]

        def ratio(part):
            nc.vector.tensor_tensor(gap[:, part], a_i[:, part], rows_sb[:, part], ALU.subtract)
            nc.scalar.activation(r_raw[:, part], gap[:, part], ACT.Exp, bias=row_shift)

        ratio(parts[0])
        half_z = col("half_z")
        z_parts = col("z_parts", BANKS)
        nc.vector.scalar_tensor_tensor(z_parts[:], z_bank[:], 0.5, lift[:], ALU.mult, ALU.mult, accum_out=half_z[:])
        ratio(parts[1])
        two_by_z = col("two_by_z")
        nc.vector.reciprocal(two_by_z[:], half_z[:])
        e2 = sb.tile([P, I], F32, name="e2")
        s2_parts = col("s2_parts", 2)
        for h, part in enumerate(parts):
            nc.vector.scalar_tensor_tensor(e2[:, part], r_raw[:, part], two_by_z[:], rows_sb[:, I + part.start : I + part.stop], ALU.mult, ALU.mult, accum_out=s2_parts[:, h : h + 1])
        p_i = sb.tile([P, I], F32, name="p_i", tag="gap_then_p_i")
        nc.scalar.activation(p_i[:], a_i[:], ACT.Exp, bias=row_shift)
        s2 = col("s2")
        nc.scalar.activation(s2[:], s2_parts[:, 0:1], ACT.Identity, bias=s2_parts[:, 1:2])
        lifted = sb.tile([P, 2, BANKS], F32, name="lifted")
        nc.gpsimd.tensor_scalar(lifted[:, 0, :], lift[:], -0.5, 0.0, ALU.mult, ALU.add)
        nc.gpsimd.tensor_scalar(lifted[:, 1, :], lift[:], 0.5 / math.sqrt(2.0), 0.0, ALU.mult, ALU.add)
        norms = sb.tile([P, 2, BANKS], F32, name="norms")
        nc.scalar.activation(norms[:], lifted[:], ACT.Copy, scale=two_by_z[:])
        nc.vector.tensor_copy(listed[:].indirect(offsets[:]), e2[:])

        s2_sq = col("s2_sq")
        nc.gpsimd.tensor_scalar(s2_sq[:], s2[:], s2[:], TINY, ALU.mult, ALU.add)
        inv_s2_sq = col("inv_s2_sq")
        nc.gpsimd.tensor_tensor(inv_s2_sq[:], s2_sq[:], minus_one[:], ALU.pow)
        inv_s2 = col("inv_s2")
        nc.gpsimd.tensor_scalar(inv_s2[:], inv_s2_sq[:], s2[:], 0.0, ALU.mult, ALU.add)
        s2_34 = col("s2_34")
        nc.gpsimd.tensor_scalar(s2_34[:], s2[:], 0.75, 0.0, ALU.mult, ALU.add)
        cross = sb.tile([P, I], F32, name="cross")
        nc.gpsimd.tensor_tensor(cross[:], p_i[:], e2[:], ALU.mult)

        scaled = sb.tile([P, 2, BANKS], F32, name="scaled")
        nc.scalar.activation(scaled[:], norms[:], ACT.Copy, scale=s2[:])

        terms = col("terms", BANKS + 2)
        quad_part = sb.tile([P, V], F32, name="quad_part")
        for b in range(BANKS):
            nc.scalar.activation(quad_part[:, bank_cols(b)], p[:, bank_cols(b)], ACT.Square, scale=scaled[:, 1, b : b + 1], accum_out=terms[:, b : b + 1])
        cross_n = sb.tile([P, I], F32, name="cross_n")
        neg_p2 = col("neg_p2")
        nc.scalar.activation(cross_n[:], cross[:], ACT.Copy, scale=norms[:, 0, BANKS - 1 : BANKS], accum_out=neg_p2[:])
        sq_parts = col("sq_parts", BANKS)
        sq_sum = col("sq_sum")
        nc.scalar.activation(sq_parts[:], terms[:, 0:BANKS], ACT.Copy, scale=inv_s2[:], accum_out=sq_sum[:])
        neg_half_c = sb.tile([P, 1], F32, name="neg_half_c", tag="c_then_squares")
        nc.scalar.activation(neg_half_c[:], neg_p2[:], ACT.Identity, scale=0.5, bias=sq_sum[:])
        offset_i = sb.tile([P, I], F32, name="offset_i")
        nc.scalar.activation(offset_i[:], e2[:], ACT.Identity, scale=-0.5, bias=neg_half_c[:])
        e1_sq = sb.tile([P, I], F32, name="e1_sq", tag="c_then_squares")
        nc.scalar.activation(e1_sq[:], e2[:], ACT.Square, scale=0.5, accum_out=terms[:, BANKS : BANKS + 1])
        nc.scalar.activation(terms[:, BANKS + 1 : BANKS + 2], neg_p2[:], ACT.Copy, scale=s2_34[:])
        terms2 = col("terms2", BANKS + 2)
        w2 = col("w2")
        nc.scalar.activation(terms2[:], terms[:], ACT.Copy, scale=2.0, accum_out=w2[:])
        lin_scale = col("lin_scale", BANKS)
        nc.scalar.activation(lin_scale[:], norms[:, 0, :], ACT.Copy, scale=w2[:])

        hda = sb.tile([P, V], F32, name="hda")
        for b in range(BANKS):
            nc.vector.scalar_tensor_tensor(hda[:, bank_cols(b)], p[:, bank_cols(b)], scaled[:, 0, b : b + 1], listed[:, bank_cols(b)], ALU.mult, ALU.add)
        looked = sb.tile([P, I], F32, name="looked")
        nc.vector.tensor_tensor(looked[:], hda[:].indirect(offsets[:]), offset_i[:], ALU.add)
        nc.vector.tensor_tensor(listed[:].indirect(offsets[:]), looked[:], e2[:], ALU.mult)

        turned = [ps.tile([P, BANK], F32, name="turned%d" % b, tag="turned%d" % b) for b in range(BANKS)]

        def add_turned(b, source, first, start, stop):
            for j in range(4):
                nc.tensor.matmul(
                    turned[b][:, j * P : (j + 1) * P],
                    source[:, first + j * P : first + (j + 1) * P],
                    ident[:],
                    start=(start and j == 0),
                    stop=(stop and j == 3),
                    is_transpose=True,
                )

        for b in range(BANKS):
            add_turned(b, rows_sb, 2 * I + b * BANK, True, False)
        for b in range(BANKS):
            add_turned(b, quad_part, b * BANK, False, False)
        lin_part = sb.tile([P, V], F32, name="lin_part")
        dense = []
        for b in range(BANKS):
            nc.scalar.activation(lin_part[:, bank_cols(b)], p[:, bank_cols(b)], ACT.Copy, scale=lin_scale[:, b : b + 1])
            add_turned(b, lin_part, b * BANK, False, True)
        for b in range(BANKS):
            turned_sb = sb.tile([P, BANK], F32, name="turned_sb%d" % b)
            nc.scalar.copy(turned_sb[:], turned[b][:])
            rows = ps.tile([P, BANK], F32, name="dense%d" % b, tag="rows%d" % b)
            for j in range(4):
                nc.tensor.transpose(rows[:, j * P : (j + 1) * P], turned_sb[:, j * P : (j + 1) * P], ident[:])
            dense.append(rows)

        first = 0
        for n, width in enumerate(STORE_WIDTHS):
            cols = slice(first, first + width)
            result = sb.tile([P, width], F32, name="result%d" % n)
            nc.vector.tensor_tensor(result[:], dense[first // BANK][:, first % BANK : first % BANK + width], listed[:, cols], ALU.add)
            queue = nc.sync if n % 2 == 0 else nc.scalar
            queue.dma_start(out=out[:, cols], in_=result[:])
            first = first + width
